import numpy as np
import ml_dtypes


def mxq(x, axis, fmt="e4m3"):
    dtype, down = {"e4m3": (ml_dtypes.float8_e4m3fn, 7), "e5m2": (ml_dtypes.float8_e5m2, 14)}[fmt]
    v = np.moveaxis(np.asarray(x, np.float32).astype(ml_dtypes.bfloat16).astype(np.float64), axis, -1)
    blocks = v.reshape(v.shape[:-1] + (-1, 32))
    amax = np.abs(blocks).max(-1, keepdims=True)
    byte = np.maximum(np.where(amax > 0, np.frexp(amax)[1] - 1 + 127, 0) - down, 1)
    scale = np.exp2(byte - 127.0)
    codes = (blocks / scale).astype(np.float32).astype(dtype).astype(np.float64)
    return np.moveaxis((codes * scale).reshape(v.shape), -1, axis)


WIDE = False


def mx_kscale(k):
    if not WIDE:
        return np.ones(k)
    levels = np.array([10, -10, 5, -5, 0])
    if k % 512:
        return np.exp2(np.random.permutation(np.resize(levels, k // 32))).repeat(32)
    a = np.empty((k // 512, 16))
    for p in range(k // 512):
        a[p, :8] = np.random.permutation(np.resize(levels, 8))
        for g in range(8):
            far = levels[np.abs(levels - a[p, g]) >= 10]
            a[p, g + 8] = far[np.random.randint(len(far))]
    return np.exp2(a.ravel()).repeat(32)


BF16 = ml_dtypes.bfloat16


def bf(x):
    return np.asarray(x, np.float32).astype(BF16)


def f64(x):
    return np.asarray(x).astype(np.float64)


N, T, D, E = 2, 512, 512, 512


def draw0():
    a, b = mx_kscale(D), mx_kscale(D)
    c = mx_kscale(T)
    return {
        "q": bf(np.random.standard_normal((N, T, D)) * a),
        "k": bf(np.random.standard_normal((N, T, D)) * c[:, None] / a),
        "zeta": bf(np.random.uniform(0.5, 1.5, (N, T)) / (c * c)),
        "lam": bf(np.random.uniform(0.5, 1.5, D)),
        "g": bf(np.random.standard_normal((N, D, E)) * b[:, None]),
        "gk": bf((1.0 + 0.2 * np.random.standard_normal(D)) * a / b),
        "gq": bf((1.0 + 0.2 * np.random.standard_normal(D)) / (a * b)),
    }


def core(q, k, zeta, lam, g, gk, gq):
    q, k, zeta, lam, g, gk, gq = f64(q), f64(k), f64(zeta), f64(lam), f64(g), f64(gk), f64(gq)
    chunk = k.shape[1]
    root_d = np.sqrt(k.shape[2])

    dg = 1.0 + lam
    x0 = q / dg

    s = (mxq(x0, 2, "e4m3") @ mxq(k, 2, "e4m3").transpose(0, 2, 1)) / root_d

    kd = gk * k / dg

    g_mx = mxq(g, 1, "e4m3")
    u = (mxq(kd, 2, "e4m3") @ g_mx) / root_d

    p = gq * x0 * (1.0 + 1.0 / dg)

    r = (mxq(p, 2, "e4m3") @ g_mx) / root_d

    sz = s * zeta[:, None, :]

    return r - (root_d / chunk) * (mxq(sz, 2, "e4m3") @ mxq(u, 1, "e4m3"))


def e4m3fn_bytes(y):
    return np.clip(np.asarray(y, np.float64), -448.0, 448.0).astype(np.float32).astype(ml_dtypes.float8_e4m3fn).view(np.uint8)


def e4m3fn_values(b):
    return np.asarray(b, np.uint8).view(ml_dtypes.float8_e4m3fn).astype(np.float64)


def setup_inputs():
    d = draw0()
    x0 = np.asarray(d['g']).astype(np.float64)
    s = (np.max(np.abs(x0), axis=(0, 2), keepdims=True) / 448.0).astype(np.float32)
    out = {}
    for k, v in d.items():
        if k == 'g':
            out['g_bytes'] = e4m3fn_bytes(x0 / s.astype(np.float64))
            out['g_scale'] = s
        else:
            out[k] = v
    return out


def reference(q, k, zeta, lam, g_bytes, g_scale, gk, gq):
    return core(q, k, zeta, lam, e4m3fn_values(g_bytes) * g_scale.astype(np.float64), gk, gq)

@@ -1,0 +1,347 @@
+import math
+from contextlib import ExitStack
+
+import concourse.mybir as mybir
+from concourse.masks import make_identity
+
+N, T, D, E = 2, 512, 512, 512
+FLOPS = N * 2 * (T * T * D + 2 * T * D * E + T * T * E)
+
+F32 = mybir.dt.float32
+BF16 = mybir.dt.bfloat16
+U32 = mybir.dt.uint32
+U8 = mybir.dt.uint8
+FP8 = mybir.dt.float8_e4m3fn
+FP8X4 = mybir.dt.float8_e4m3fn_x4
+MULT = mybir.AluOpType.mult
+ADD = mybir.AluOpType.add
+COPY = mybir.ActivationFunctionType.Copy
+
+P = 128
+PACK = 4
+HALF = 256
+CHUNK = 128
+INV_ROOT_D = 1.0 / math.sqrt(D)
+
+LATE = (("kd", 1), ("q", 0), ("q", 1))
+
+assert T == D == E == P * PACK
+
+
+def tile_diagonalpreconditionedstepread_kernel(tc, q, k, zeta, lam, g_bytes, g_scale, gk, gq, out):
+    nc = tc.nc
+    with ExitStack() as ctx:
+        keep = ctx.enter_context(tc.tile_pool(name="keep", bufs=1))
+        psum = ctx.enter_context(tc.psum_pool(name="psum", bufs=1))
+        ctx.enter_context(tc.manual_schedule())
+
+        def sbuf(name, shape, dtype, tag=None):
+            return keep.tile(shape, dtype, name=name, tag=tag or name, align_bytes=64)
+
+        def bank(index, name):
+            return psum.tile([P, 512], F32, name=name, tag="bank%d" % index)
+
+        def mx_operand(name):
+            return sbuf(name + "_codes", [P, 512], U32), sbuf(name + "_scales", [P, 512], U8)
+
+        lam_sb = sbuf("lam_sb", [P, PACK], BF16)
+        gk_sb = sbuf("gk_sb", [P, PACK], BF16)
+        gq_sb = sbuf("gq_sb", [P, PACK], BF16)
+        gs_sb = sbuf("gs_sb", [P, PACK], F32)
+        zeta_sb = sbuf("zeta_sb", [P, N, PACK], BF16)
+        nc.scalar.dma_start(out=lam_sb[:], in_=lam.rearrange("(p t) -> p t", t=PACK))
+        nc.scalar.dma_start(out=gk_sb[:], in_=gk.rearrange("(p t) -> p t", t=PACK))
+        nc.scalar.dma_start(out=gq_sb[:], in_=gq.rearrange("(p t) -> p t", t=PACK))
+        nc.scalar.dma_start(out=gs_sb[:], in_=g_scale.rearrange("a (p t) b -> p (a t b)", t=PACK))
+
+        rows = {}
+        g_raw = {}
+
+        def load_rows(src, name, n, h):
+            t = sbuf("%s_rows%d%d" % (name, n, h), [P, 2 * D], BF16)
+            nc.sync.dma_start(out=t[:], in_=src[n].rearrange("(m h j) d -> h m (j d)", h=2, j=2)[h])
+            rows[name, n, h] = t
+
+        def load_g(n):
+            t = sbuf("g_raw%d" % n, [P, PACK * E], U8)
+            nc.sync.dma_start(out=t[:], in_=g_bytes[n].rearrange("(p t) e -> p (t e)", t=PACK))
+            g_raw[n] = t
+
+        def load_zeta():
+            nc.sync.dma_start(out=zeta_sb[:], in_=zeta.rearrange("n (p j) -> p n j", j=PACK))
+
+        ident = sbuf("ident", [P, P], F32)
+        make_identity(nc, ident[:])
+        warm = sbuf("warm", [P, 1], F32)
+        nc.scalar.activation(out=warm[:], in_=ident[:, 0:1], func=COPY, scale=1.0)
+
+        dg = sbuf("dg", [P, PACK], F32)
+        c_x = sbuf("c_x", [P, PACK], F32)
+        c_k = sbuf("c_k", [P, PACK], F32)
+        c_t = sbuf("c_t", [P, PACK], F32)
+        c_p = sbuf("c_p", [P, PACK], F32)
+        c_z = sbuf("c_z", [P, N, PACK], F32)
+
+        def factors():
+            nc.vector.tensor_scalar(out=dg[:], in0=lam_sb[:], scalar1=1.0, scalar2=None, op0=ADD)
+            nc.vector.reciprocal(out=c_x[:], in_=dg[:])
+            nc.vector.tensor_tensor(out=c_k[:], in0=c_x[:], in1=gk_sb[:], op=MULT)
+            nc.vector.scalar_tensor_tensor(out=c_t[:], in0=c_x[:], scalar=1.0, in1=c_x[:], op0=ADD, op1=MULT)
+            nc.vector.tensor_tensor(out=c_p[:], in0=c_t[:], in1=gq_sb[:], op=MULT)
+
+        def zeta_factor():
+            nc.vector.tensor_scalar(out=c_z[:], in0=zeta_sb[:], scalar1=INV_ROOT_D, scalar2=None, op0=MULT)
+
+        wide = {}
+        mx = {}
+        for n in range(N):
+            for name in ("k", "x", "p", "kd", "g", "sz", "u"):
+                mx[name, n] = mx_operand("%s%d" % (name, n))
+            for name in ("k", "q", "x", "p", "sz", "u", "kd", "g"):
+                if (name, n) not in LATE:
+                    wide[name, n] = sbuf("%s_wide%d" % (name, n), [P, 512 * PACK], BF16)
+        planes = {n: sbuf("g_planes%d" % n, [P, PACK, E], BF16) for n in range(N)}
+        turned = {}
+        sums = {}
+
+        def turn(name, n, h, index):
+            b = bank(index, "%s_turned%d%d" % (name, n, h))
+            words = rows[name, n, h][:].bitcast(F32)
+            for j in range(2):
+                for u in range(2):
+                    nc.tensor.transpose(
+                        b[:, HALF * u + P * j : HALF * u + P * (j + 1)],
+                        words[:, HALF * j + u : HALF * (j + 1) : 2],
+                        ident[:],
+                    )
+            turned[name, n, h] = b
+
+        def half(name, n, h):
+            return wide[name, n][:, HALF * PACK * h : HALF * PACK * (h + 1)]
+
+        def copy_k(n, h):
+            nc.scalar.copy(
+                out=half("k", n, h).bitcast(F32).rearrange("p (c u) -> p c u", u=2),
+                in_=turned["k", n, h][:].rearrange("p (u c) -> p c u", u=2),
+            )
+
+        def scale_turned(dst, src, factor, n, h):
+            nc.vector.tensor_tensor(
+                out=half(dst, n, h).rearrange("p (c u e) -> p c u e", u=2, e=2),
+                in0=turned[src, n, h][:].bitcast(BF16).rearrange("p (u c e) -> p c u e", u=2, e=2),
+                in1=factor[:].rearrange("p (u e) -> p u e", u=2).unsqueeze(1).to_broadcast([P, HALF, 2, 2]),
+                op=MULT,
+            )
+
+        def kd_on_gpsimd(n, h):
+            nc.gpsimd.tensor_tensor(
+                out=half("kd", n, h).rearrange("p (c t) -> p c t", t=PACK),
+                in0=half("k", n, h).rearrange("p (c t) -> p c t", t=PACK),
+                in1=c_k[:].unsqueeze(1).to_broadcast([P, HALF, PACK]),
+                op=MULT,
+            )
+
+        def copy_q(n, h):
+            nc.scalar.copy(
+                out=half("q", n, h).bitcast(F32).rearrange("p (c u) -> p c u", u=2),
+                in_=turned["q", n, h][:].rearrange("p (u c) -> p c u", u=2),
+            )
+
+        def p_on_gpsimd(n, h):
+            nc.gpsimd.tensor_tensor(
+                out=half("p", n, h).rearrange("p (c t) -> p c t", t=PACK),
+                in0=half("q", n, h).rearrange("p (c t) -> p c t", t=PACK),
+                in1=c_p[:].unsqueeze(1).to_broadcast([P, HALF, PACK]),
+                op=MULT,
+            )
+
+        def widen_g(n, t, eng="S"):
+            src = g_raw[n][:, E * t : E * (t + 1)].bitcast(FP8)
+            if eng == "S":
+                nc.scalar.activation(out=planes[n][:, t, :], in_=src, func=COPY, scale=gs_sb[:, t : t + 1])
+            else:
+                nc.vector.tensor_scalar(
+                    out=planes[n][:, t, :], in0=src, scalar1=gs_sb[:, t : t + 1], scalar2=None, op0=MULT
+                )
+
+        def interleave_g(n, c0=0, c1=512, eng="S"):
+            dst = wide["g", n][:, PACK * c0 : PACK * c1].rearrange("p (c i t) -> p c t i", i=4, t=PACK)
+            src = planes[n][:, :, c0:c1].rearrange("p t (c i) -> p c t i", i=4)
+            if eng == "S":
+                nc.scalar.copy(out=dst, in_=src)
+            elif eng == "V":
+                nc.vector.tensor_copy(out=dst, in_=src)
+            else:
+                nc.gpsimd.tensor_scalar(out=dst, in0=src, scalar1=1.0, scalar2=0.0, op0=MULT, op1=ADD)
+
+        def quantize(name, n, c0=0, c1=512):
+            codes, scales = mx[name, n]
+            nc.vector.quantize_mx(
+                out=codes[:, c0:c1].bitcast(FP8X4),
+                scales=scales[:, c0:c1],
+                in_=wide[name, n][:, PACK * c0 : PACK * c1],
+            )
+
+        def mx_pass(dst, lhs, rhs, n, m_cols, n_cols, start, stop):
+            nc.tensor.matmul_mx(
+                out=dst,
+                lhsT=mx[lhs, n][0][:, m_cols].bitcast(FP8X4),
+                lhsT_scale=mx[lhs, n][1][:, m_cols],
+                rhs=mx[rhs, n][0][:, n_cols].bitcast(FP8X4),
+                rhs_scale=mx[rhs, n][1][:, n_cols],
+                start=start,
+                stop=stop,
+            )
+
+        def cols(b):
+            return slice(CHUNK * b, CHUNK * (b + 1))
+
+        def over_keys(name, lhs, rhs, n, b, index):
+            acc = bank(index, "%s_sums%d%d" % (name, n, b))
+            for j in range(PACK):
+                mx_pass(acc[:, cols(j)], lhs, rhs, n, cols(j), cols(b), True, True)
+            sums[name, n, b] = acc
+
+        def chunk(name, n, b):
+            return wide[name, n][:, CHUNK * PACK * b : CHUNK * PACK * (b + 1)].rearrange("p (c j) -> p c j", j=PACK)
+
+        def make_sz(n, b):
+            nc.vector.tensor_tensor(
+                out=chunk("sz", n, b),
+                in0=sums["s", n, b][:].rearrange("p (j c) -> p c j", j=PACK),
+                in1=c_z[:, n, :].unsqueeze(1).to_broadcast([P, CHUNK, PACK]),
+                op=MULT,
+            )
+
+        z_planes = {}
+
+        def sz_planes(n, b):
+            pl = sbuf("z_planes%d%d" % (n, b), [P, PACK, CHUNK], BF16)
+            for j in range(PACK):
+                nc.scalar.activation(
+                    out=pl[:, j, :], in_=sums["s", n, b][:, cols(j)], func=COPY, scale=c_z[:, n, j : j + 1]
+                )
+            z_planes[n, b] = pl
+
+        def sz_interleave(n, b):
+            nc.vector.tensor_copy(
+                out=chunk("sz", n, b).rearrange("p (c i) t -> p c t i", i=4),
+                in_=z_planes[n, b][:].rearrange("p t (c i) -> p c t i", i=4),
+            )
+
+        def scaled_copy(dst, src, factor, eng):
+            if eng == "S":
+                nc.scalar.activation(out=dst, in_=src, func=COPY, scale=factor)
+            else:
+                nc.vector.tensor_scalar(out=dst, in0=src, scalar1=factor, scalar2=None, op0=MULT)
+
+        def make_u(n, b, eng="S"):
+            scaled_copy(chunk("u", n, b), sums["u", n, b][:].rearrange("p (j c) -> p c j", j=PACK), -INV_ROOT_D, eng)
+
+        def out_open(n, b, index):
+            acc = bank(index, "out_sums%d%d" % (n, b))
+            mx_pass(acc[:], "p", "g", n, cols(b), slice(0, E), True, False)
+            sums["out", n, b] = acc
+
+        def out_close(n, b):
+            mx_pass(sums["out", n, b][:], "sz", "u", n, cols(b), slice(0, E), False, True)
+
+        def out_product(n, b, index):
+            out_open(n, b, index)
+            out_close(n, b)
+
+        def store(n, b, eng="S"):
+            res = sbuf("res%d%d" % (n, b), [P, E], F32)
+            scaled_copy(res[:], sums["out", n, b][:], INV_ROOT_D, eng)
+            nc.sync.dma_start(out=out[n].rearrange("(m j) e -> j m e", j=PACK)[b], in_=res[:])
+
+        A, B, C, DD, EE, FF, G, H = range(8)
+        for n in range(N):
+            for name, src in (("k", k), ("q", q)):
+                for h in range(2):
+                    load_rows(src, name, n, h)
+            load_g(n)
+            if n == 0:
+                load_zeta()
+        factors()
+        turn("k", 0, 0, A)
+        turn("k", 0, 1, B)
+        turn("q", 0, 0, C)
+        turn("q", 0, 1, DD)
+        scale_turned("kd", "k", c_k, 0, 0)
+        copy_k(0, 1)
+        copy_k(0, 0)
+        kd_on_gpsimd(0, 1)
+        for t in range(PACK):
+            widen_g(0, t)
+        scale_turned("x", "q", c_x, 0, 0)
+        scale_turned("x", "q", c_x, 0, 1)
+        scale_turned("p", "q", c_p, 0, 0)
+        interleave_g(0)
+        turn("k", 1, 0, A)
+        turn("k", 1, 1, B)
+        turn("q", 1, 0, C)
+        quantize("kd", 0)
+        quantize("k", 0)
+        quantize("x", 0)
+        zeta_factor()
+        for b, index in enumerate((EE, FF, G, H)):
+            over_keys("s", "k", "x", 0, b, index)
+        scale_turned("p", "q", c_p, 0, 1)
+        turn("q", 1, 1, DD)
+        copy_k(1, 0)
+        copy_k(1, 1)
+        quantize("g", 0)
+        wide["kd", 1] = sbuf("kd_wide1", [P, 512 * PACK], BF16, tag="g_wide0")
+        kd_on_gpsimd(1, 0)
+        kd_on_gpsimd(1, 1)
+        for t in range(PACK):
+            widen_g(1, t)
+        for b in range(PACK):
+            over_keys("u", "kd", "g", 0, b, (A, B)[b % 2])
+            make_u(0, b)
+            make_sz(0, b)
+        interleave_g(1)
+        scale_turned("x", "q", c_x, 1, 0)
+        scale_turned("x", "q", c_x, 1, 1)
+        scale_turned("p", "q", c_p, 1, 0)
+        quantize("kd", 1)
+        quantize("g", 1)
+        quantize("k", 1)
+        quantize("x", 1)
+        quantize("sz", 0)
+        quantize("p", 0)
+        quantize("u", 0)
+        over_keys("u", "kd", "g", 1, 0, A)
+        over_keys("u", "kd", "g", 1, 1, B)
+        over_keys("u", "kd", "g", 1, 2, EE)
+        over_keys("u", "kd", "g", 1, 3, FF)
+        for b in range(PACK):
+            make_u(1, b)
+        for b, index in enumerate((G, H, C, A)):
+            over_keys("s", "k", "x", 1, b, index)
+        for b in range(PACK):
+            out_product(0, b, (B, EE, FF)[b % 3])
+            store(0, b)
+        scale_turned("p", "q", c_p, 1, 1)
+        make_sz(1, 0)
+        make_sz(1, 1)
+        quantize("p", 1)
+        quantize("u", 1)
+        quantize("sz", 1, 0, 256)
+        make_sz(1, 2)
+        out_open(1, 0, DD)
+        out_open(1, 1, G)
+        out_open(1, 2, H)
+        out_open(1, 3, EE)
+        out_close(1, 0)
+        out_close(1, 1)
+        make_sz(1, 3)
+        store(1, 0)
+        store(1, 1)
+        quantize("sz", 1, 256, 384)
+        quantize("sz", 1, 384, 512)
+        out_close(1, 2)
+        out_close(1, 3)
+        store(1, 2)
+        store(1, 3, "V")

@@ -255,93 +255,166 @@ def tile_diagonalpreconditionedstepread_kernel(tc, q, k, zeta, lam, g_bytes, g_s
             scaled_copy(res[:], sums["out", n, b][:], INV_ROOT_D, eng)
             nc.sync.dma_start(out=out[n].rearrange("(m j) e -> j m e", j=PACK)[b], in_=res[:])
 
+        t_planes = {}
+
+        def planes_turned(dst, src, factor, n, h):
+            pl = sbuf("%s_planes%d%d" % (dst, n, h), [P, PACK, HALF], BF16)
+            view = turned[src, n, h][:].bitcast(BF16).rearrange("p (u c e) -> p u e c", u=2, e=2)
+            for t in range(PACK):
+                nc.scalar.activation(
+                    out=pl[:, t, :], in_=view[:, t // 2, t % 2, :], func=COPY, scale=factor[:, t : t + 1]
+                )
+            t_planes[dst, n, h] = pl
+
+        def interleave_turned(dst, n, h):
+            nc.vector.tensor_copy(
+                out=half(dst, n, h).rearrange("p (c i t) -> p c t i", i=4, t=PACK),
+                in_=t_planes[dst, n, h][:].rearrange("p t (c i) -> p c t i", i=4),
+            )
+
+        def out_open_half(n, b, hh, index):
+            acc = bank(index, "out_sums%d%d%d" % (n, b, hh))
+            mx_pass(acc[:, :HALF], "p", "g", n, cols(b), slice(HALF * hh, HALF * (hh + 1)), True, False)
+            sums["out", n, b, hh] = acc
+
+        def out_close_half(n, b, hh):
+            acc = sums["out", n, b, hh]
+            mx_pass(acc[:, :HALF], "sz", "u", n, cols(b), slice(HALF * hh, HALF * (hh + 1)), False, True)
+
+        def store_half(n, b, hh, eng="S"):
+            res = sbuf("res%d%d%d" % (n, b, hh), [P, HALF], F32)
+            scaled_copy(res[:], sums["out", n, b, hh][:, :HALF], INV_ROOT_D, eng)
+            dst = out[n].rearrange("(m j) e -> j m e", j=PACK)[b]
+            nc.sync.dma_start(out=dst[:, HALF * hh : HALF * (hh + 1)], in_=res[:])
+
+        def warm_up(index, count, width):
+            zeros = sbuf("warm_zeros", [P, width], F32)
+            nc.vector.memset(zeros[:], 0.0)
+            acc = bank(index, "warm_sums")
+            for i in range(count):
+                nc.tensor.matmul(acc[:, :width], lhsT=zeros[:, :P], rhs=zeros[:], start=True, stop=True)
+
+        def rewarm(index, count):
+            src = half("kd", 1, 1)
+            acc = bank(index, "rewarm_sums")
+            for i in range(count):
+                nc.tensor.matmul(acc[:], lhsT=src[:, :P], rhs=src[:, :512], start=True, stop=True)
+
         A, B, C, DD, EE, FF, G, H = range(8)
         for n in range(N):
-            for name, src in (("k", k), ("q", q)):
-                for h in range(2):
-                    load_rows(src, name, n, h)
+            load_rows(q, "q", n, 0)
+            load_rows(k, "k", n, 0)
+            load_rows(k, "k", n, 1)
+            load_rows(q, "q", n, 1)
             load_g(n)
             if n == 0:
                 load_zeta()
+        warm_up(H, 5, 128)
         factors()
+        turn("q", 0, 0, C)
         turn("k", 0, 0, A)
         turn("k", 0, 1, B)
-        turn("q", 0, 0, C)
         turn("q", 0, 1, DD)
-        scale_turned("kd", "k", c_k, 0, 0)
-        copy_k(0, 1)
         copy_k(0, 0)
-        kd_on_gpsimd(0, 1)
+        copy_k(0, 1)
+        kd_on_gpsimd(0, 0)
         for t in range(PACK):
             widen_g(0, t)
-        scale_turned("x", "q", c_x, 0, 0)
-        scale_turned("x", "q", c_x, 0, 1)
-        scale_turned("p", "q", c_p, 0, 0)
         interleave_g(0)
+        scale_turned("x", "q", c_x, 0, 0)
+        scale_turned("p", "q", c_p, 0, 0)
+        scale_turned("kd", "k", c_k, 0, 1)
+        scale_turned("x", "q", c_x, 0, 1)
         turn("k", 1, 0, A)
         turn("k", 1, 1, B)
         turn("q", 1, 0, C)
+        copy_k(1, 0)
+        copy_k(1, 1)
         quantize("kd", 0)
         quantize("k", 0)
         quantize("x", 0)
         zeta_factor()
-        for b, index in enumerate((EE, FF, G, H)):
-            over_keys("s", "k", "x", 0, b, index)
-        scale_turned("p", "q", c_p, 0, 1)
-        turn("q", 1, 1, DD)
-        copy_k(1, 0)
-        copy_k(1, 1)
         quantize("g", 0)
         wide["kd", 1] = sbuf("kd_wide1", [P, 512 * PACK], BF16, tag="g_wide0")
         kd_on_gpsimd(1, 0)
         kd_on_gpsimd(1, 1)
-        for t in range(PACK):
-            widen_g(1, t)
-        for b in range(PACK):
-            over_keys("u", "kd", "g", 0, b, (A, B)[b % 2])
-            make_u(0, b)
-            make_sz(0, b)
-        interleave_g(1)
+        widen_g(1, 0)
+        widen_g(1, 1)
+        over_keys("s", "k", "x", 0, 0, EE)
+        over_keys("s", "k", "x", 0, 1, FF)
+        over_keys("u", "kd", "g", 0, 0, A)
+        over_keys("u", "kd", "g", 0, 1, B)
+        over_keys("s", "k", "x", 0, 2, G)
+        over_keys("s", "k", "x", 0, 3, H)
+        scale_turned("p", "q", c_p, 0, 1)
+        make_u(0, 0)
+        make_u(0, 1)
+        over_keys("u", "kd", "g", 0, 2, A)
+        over_keys("u", "kd", "g", 0, 3, B)
+        make_u(0, 2)
+        make_u(0, 3)
+        turn("q", 1, 1, DD)
         scale_turned("x", "q", c_x, 1, 0)
+        for b in range(PACK):
+            make_sz(0, b)
         scale_turned("x", "q", c_x, 1, 1)
-        scale_turned("p", "q", c_p, 1, 0)
+        widen_g(1, 2)
+        widen_g(1, 3)
+        interleave_g(1)
+        rewarm(A, 3)
         quantize("kd", 1)
+        quantize("p", 0)
+        quantize("sz", 0)
+        quantize("u", 0)
         quantize("g", 1)
         quantize("k", 1)
         quantize("x", 1)
-        quantize("sz", 0)
-        quantize("p", 0)
-        quantize("u", 0)
+        for b, index in enumerate((EE, FF, G, H)):
+            out_open(0, b, index)
+        for b in range(PACK):
+            out_close(0, b)
         over_keys("u", "kd", "g", 1, 0, A)
         over_keys("u", "kd", "g", 1, 1, B)
+        store(0, 0)
+        store(0, 1)
         over_keys("u", "kd", "g", 1, 2, EE)
         over_keys("u", "kd", "g", 1, 3, FF)
-        for b in range(PACK):
-            make_u(1, b)
-        for b, index in enumerate((G, H, C, A)):
-            over_keys("s", "k", "x", 1, b, index)
-        for b in range(PACK):
-            out_product(0, b, (B, EE, FF)[b % 3])
-            store(0, b)
+        make_u(1, 0)
+        make_u(1, 1)
+        over_keys("s", "k", "x", 1, 0, A)
+        over_keys("s", "k", "x", 1, 1, B)
+        make_u(1, 2)
+        make_u(1, 3)
+        over_keys("s", "k", "x", 1, 2, EE)
+        over_keys("s", "k", "x", 1, 3, FF)
+        store(0, 2)
+        store(0, 3)
+        scale_turned("p", "q", c_p, 1, 0)
         scale_turned("p", "q", c_p, 1, 1)
         make_sz(1, 0)
-        make_sz(1, 1)
         quantize("p", 1)
         quantize("u", 1)
-        quantize("sz", 1, 0, 256)
-        make_sz(1, 2)
-        out_open(1, 0, DD)
-        out_open(1, 1, G)
-        out_open(1, 2, H)
-        out_open(1, 3, EE)
+        quantize("sz", 1, 0, 128)
+        make_sz(1, 1)
+        sz_planes(1, 2)
+        sz_planes(1, 3)
+        out_open(1, 0, C)
+        out_open(1, 1, DD)
         out_close(1, 0)
-        out_close(1, 1)
-        make_sz(1, 3)
-        store(1, 0)
-        store(1, 1)
+        out_open(1, 2, G)
+        out_open_half(1, 3, 0, H)
+        out_open_half(1, 3, 1, A)
+        sz_interleave(1, 2)
+        quantize("sz", 1, 128, 256)
+        sz_interleave(1, 3)
         quantize("sz", 1, 256, 384)
         quantize("sz", 1, 384, 512)
+        out_close(1, 1)
         out_close(1, 2)
-        out_close(1, 3)
-        store(1, 2)
-        store(1, 3, "V")
+        out_close_half(1, 3, 0)
+        out_close_half(1, 3, 1)
+        store(1, 0)
+        store(1, 1)
+        store(1, 2, "V")
+        store_half(1, 3, 0)
+        store_half(1, 3, 1, "V")

@@ -50,17 +50,23 @@ def tile_diagonalpreconditionedstepread_kernel(tc, q, k, zeta, lam, g_bytes, g_s
         gs_sb = sbuf("gs_sb", [P, PACK], F32)
         zeta_sb = sbuf("zeta_sb", [P, N, PACK], BF16)
         nc.scalar.dma_start(out=lam_sb[:], in_=lam.rearrange("(p t) -> p t", t=PACK))
-        nc.scalar.dma_start(out=gk_sb[:], in_=gk.rearrange("(p t) -> p t", t=PACK))
         nc.scalar.dma_start(out=gq_sb[:], in_=gq.rearrange("(p t) -> p t", t=PACK))
+
         nc.scalar.dma_start(out=gs_sb[:], in_=g_scale.rearrange("a (p t) b -> p (a t b)", t=PACK))
 
         rows = {}
         g_raw = {}
 
-        def load_rows(src, name, n, h):
-            t = sbuf("%s_rows%d%d" % (name, n, h), [P, 2 * D], BF16)
-            nc.sync.dma_start(out=t[:], in_=src[n].rearrange("(m h j) d -> h m (j d)", h=2, j=2)[h])
-            rows[name, n, h] = t
+        def load_rows(src, name, n, j0, j1):
+            t = sbuf("%s_rows%d%d" % (name, n, j0), [P, (j1 - j0) * D], BF16)
+            nc.sync.dma_start(out=t[:], in_=src[n].rearrange("(m j) d -> m (j d)", j=PACK)[:, D * j0 : D * j1])
+            rows[name, n, j0] = t
+
+        def load_small(which):
+            if which == "gk":
+                nc.sync.dma_start(out=gk_sb[:], in_=gk.rearrange("(p t) -> p t", t=PACK))
+            else:
+                nc.sync.dma_start(out=gs_sb[:], in_=g_scale.rearrange("a (p t) b -> p (a t b)", t=PACK))
 
         def load_g(n):
             t = sbuf("g_raw%d" % n, [P, PACK * E], U8)
@@ -70,6 +76,8 @@ def tile_diagonalpreconditionedstepread_kernel(tc, q, k, zeta, lam, g_bytes, g_s
         def load_zeta():
             nc.sync.dma_start(out=zeta_sb[:], in_=zeta.rearrange("n (p j) -> p n j", j=PACK))
 
+        zeros = sbuf("warm_zeros", [P, P], F32)
+        nc.gpsimd.memset(zeros[:], 0.0)
         ident = sbuf("ident", [P, P], F32)
         make_identity(nc, ident[:])
         warm = sbuf("warm", [P, 1], F32)
@@ -82,12 +90,18 @@ def tile_diagonalpreconditionedstepread_kernel(tc, q, k, zeta, lam, g_bytes, g_s
         c_p = sbuf("c_p", [P, PACK], F32)
         c_z = sbuf("c_z", [P, N, PACK], F32)
 
-        def factors():
+        def f_x():
             nc.vector.tensor_scalar(out=dg[:], in0=lam_sb[:], scalar1=1.0, scalar2=None, op0=ADD)
             nc.vector.reciprocal(out=c_x[:], in_=dg[:])
-            nc.vector.tensor_tensor(out=c_k[:], in0=c_x[:], in1=gk_sb[:], op=MULT)
+
+        def f_t():
             nc.vector.scalar_tensor_tensor(out=c_t[:], in0=c_x[:], scalar=1.0, in1=c_x[:], op0=ADD, op1=MULT)
+
+        def f_p():
             nc.vector.tensor_tensor(out=c_p[:], in0=c_t[:], in1=gq_sb[:], op=MULT)
+
+        def f_k():
+            nc.gpsimd.tensor_tensor(out=c_k[:], in0=c_x[:], in1=gk_sb[:], op=MULT)
 
         def zeta_factor():
             nc.vector.tensor_scalar(out=c_z[:], in0=zeta_sb[:], scalar1=INV_ROOT_D, scalar2=None, op0=MULT)
@@ -104,55 +118,65 @@ def tile_diagonalpreconditionedstepread_kernel(tc, q, k, zeta, lam, g_bytes, g_s
         turned = {}
         sums = {}
 
-        def turn(name, n, h, index):
-            b = bank(index, "%s_turned%d%d" % (name, n, h))
-            words = rows[name, n, h][:].bitcast(F32)
-            for j in range(2):
+        def turn(name, n, j0, j1, index):
+            b = bank(index, "%s_turned%d%d" % (name, n, j0))
+            words = rows[name, n, j0][:].bitcast(F32)
+            view = b[:].rearrange("p (u c) -> p c u", u=2)
+            for j in range(j1 - j0):
                 for u in range(2):
                     nc.tensor.transpose(
                         b[:, HALF * u + P * j : HALF * u + P * (j + 1)],
                         words[:, HALF * j + u : HALF * (j + 1) : 2],
                         ident[:],
                     )
-            turned[name, n, h] = b
+                turned[name, n, j0 + j] = (b, j)
 
-        def half(name, n, h):
-            return wide[name, n][:, HALF * PACK * h : HALF * PACK * (h + 1)]
+        def slots(name, n, j0, j1):
+            return wide[name, n][:, P * PACK * j0 : P * PACK * j1]
 
-        def copy_k(n, h):
+        def turned_values(name, n, j0, j1):
+            b, first = turned[name, n, j0]
+            view = b[:].bitcast(BF16).rearrange("p (u c e) -> p c u e", u=2, e=2)
+            return view[:, P * first : P * (first + j1 - j0)]
+
+        def copy_k(n, j0, j1):
+            b, first = turned["k", n, j0]
             nc.scalar.copy(
-                out=half("k", n, h).bitcast(F32).rearrange("p (c u) -> p c u", u=2),
-                in_=turned["k", n, h][:].rearrange("p (u c) -> p c u", u=2),
+                out=slots("k", n, j0, j1).bitcast(F32).rearrange("p (c u) -> p c u", u=2),
+                in_=b[:].rearrange("p (u c) -> p c u", u=2)[:, P * first : P * (first + j1 - j0)],
             )
 
-        def scale_turned(dst, src, factor, n, h):
+        def scale_turned(dst, src, factor, n, j0, j1):
             nc.vector.tensor_tensor(
-                out=half(dst, n, h).rearrange("p (c u e) -> p c u e", u=2, e=2),
-                in0=turned[src, n, h][:].bitcast(BF16).rearrange("p (u c e) -> p c u e", u=2, e=2),
-                in1=factor[:].rearrange("p (u e) -> p u e", u=2).unsqueeze(1).to_broadcast([P, HALF, 2, 2]),
+                out=slots(dst, n, j0, j1).rearrange("p (c u e) -> p c u e", u=2, e=2),
+                in0=turned_values(src, n, j0, j1),
+                in1=factor[:].rearrange("p (u e) -> p u e", u=2).unsqueeze(1).to_broadcast([P, P * (j1 - j0), 2, 2]),
                 op=MULT,
             )
 
-        def kd_on_gpsimd(n, h):
+        def kd_on_gpsimd(n, j0, j1):
             nc.gpsimd.tensor_tensor(
-                out=half("kd", n, h).rearrange("p (c t) -> p c t", t=PACK),
-                in0=half("k", n, h).rearrange("p (c t) -> p c t", t=PACK),
-                in1=c_k[:].unsqueeze(1).to_broadcast([P, HALF, PACK]),
+                out=slots("kd", n, j0, j1).rearrange("p (c t) -> p c t", t=PACK),
+                in0=slots("k", n, j0, j1).rearrange("p (c t) -> p c t", t=PACK),
+                in1=c_k[:].unsqueeze(1).to_broadcast([P, P * (j1 - j0), PACK]),
                 op=MULT,
             )
 
-        def copy_q(n, h):
-            nc.scalar.copy(
-                out=half("q", n, h).bitcast(F32).rearrange("p (c u) -> p c u", u=2),
-                in_=turned["q", n, h][:].rearrange("p (u c) -> p c u", u=2),
-            )
+        t_planes = {}
 
-        def p_on_gpsimd(n, h):
-            nc.gpsimd.tensor_tensor(
-                out=half("p", n, h).rearrange("p (c t) -> p c t", t=PACK),
-                in0=half("q", n, h).rearrange("p (c t) -> p c t", t=PACK),
-                in1=c_p[:].unsqueeze(1).to_broadcast([P, HALF, PACK]),
-                op=MULT,
+        def p_planes(n, j0, j1):
+            pl = sbuf("p_planes%d%d" % (n, j0), [P, PACK, P * (j1 - j0)], BF16)
+            view = turned_values("q", n, j0, j1)
+            for t in range(PACK):
+                nc.scalar.activation(
+                    out=pl[:, t, :], in_=view[:, :, t // 2, t % 2], func=COPY, scale=c_p[:, t : t + 1]
+                )
+            t_planes[n, j0] = pl
+
+        def p_interleave(n, j0, j1):
+            nc.vector.tensor_copy(
+                out=slots("p", n, j0, j1).rearrange("p (c i t) -> p c t i", i=4, t=PACK),
+                in_=t_planes[n, j0][:].rearrange("p t (c i) -> p c t i", i=4),
             )
 
         def widen_g(n, t, eng="S"):
@@ -174,12 +198,12 @@ def tile_diagonalpreconditionedstepread_kernel(tc, q, k, zeta, lam, g_bytes, g_s
             else:
                 nc.gpsimd.tensor_scalar(out=dst, in0=src, scalar1=1.0, scalar2=0.0, op0=MULT, op1=ADD)
 
-        def quantize(name, n, c0=0, c1=512):
+        def quantize(name, n, j0=0, j1=PACK):
             codes, scales = mx[name, n]
             nc.vector.quantize_mx(
-                out=codes[:, c0:c1].bitcast(FP8X4),
-                scales=scales[:, c0:c1],
-                in_=wide[name, n][:, PACK * c0 : PACK * c1],
+                out=codes[:, P * j0 : P * j1].bitcast(FP8X4),
+                scales=scales[:, P * j0 : P * j1],
+                in_=slots(name, n, j0, j1),
             )
 
         def mx_pass(dst, lhs, rhs, n, m_cols, n_cols, start, stop):
@@ -255,23 +279,6 @@ def tile_diagonalpreconditionedstepread_kernel(tc, q, k, zeta, lam, g_bytes, g_s
             scaled_copy(res[:], sums["out", n, b][:], INV_ROOT_D, eng)
             nc.sync.dma_start(out=out[n].rearrange("(m j) e -> j m e", j=PACK)[b], in_=res[:])
 
-        t_planes = {}
-
-        def planes_turned(dst, src, factor, n, h):
-            pl = sbuf("%s_planes%d%d" % (dst, n, h), [P, PACK, HALF], BF16)
-            view = turned[src, n, h][:].bitcast(BF16).rearrange("p (u c e) -> p u e c", u=2, e=2)
-            for t in range(PACK):
-                nc.scalar.activation(
-                    out=pl[:, t, :], in_=view[:, t // 2, t % 2, :], func=COPY, scale=factor[:, t : t + 1]
-                )
-            t_planes[dst, n, h] = pl
-
-        def interleave_turned(dst, n, h):
-            nc.vector.tensor_copy(
-                out=half(dst, n, h).rearrange("p (c i t) -> p c t i", i=4, t=PACK),
-                in_=t_planes[dst, n, h][:].rearrange("p t (c i) -> p c t i", i=4),
-            )
-
         def out_open_half(n, b, hh, index):
             acc = bank(index, "out_sums%d%d%d" % (n, b, hh))
             mx_pass(acc[:, :HALF], "p", "g", n, cols(b), slice(HALF * hh, HALF * (hh + 1)), True, False)
@@ -288,79 +295,95 @@ def tile_diagonalpreconditionedstepread_kernel(tc, q, k, zeta, lam, g_bytes, g_s
             nc.sync.dma_start(out=dst[:, HALF * hh : HALF * (hh + 1)], in_=res[:])
 
         def warm_up(index, count, width):
-            zeros = sbuf("warm_zeros", [P, width], F32)
-            nc.vector.memset(zeros[:], 0.0)
-            acc = bank(index, "warm_sums")
+            acc = bank(index, "warm_sums%d" % count)
             for i in range(count):
-                nc.tensor.matmul(acc[:, :width], lhsT=zeros[:, :P], rhs=zeros[:], start=True, stop=True)
+                nc.tensor.matmul(acc[:, :width], lhsT=zeros[:], rhs=zeros[:], start=True, stop=True)
 
         def rewarm(index, count):
-            src = half("kd", 1, 1)
+            src = slots("kd", 1, 2, 4)
             acc = bank(index, "rewarm_sums")
             for i in range(count):
                 nc.tensor.matmul(acc[:], lhsT=src[:, :P], rhs=src[:, :512], start=True, stop=True)
 
         A, B, C, DD, EE, FF, G, H = range(8)
-        for n in range(N):
-            load_rows(q, "q", n, 0)
-            load_rows(k, "k", n, 0)
-            load_rows(k, "k", n, 1)
-            load_rows(q, "q", n, 1)
-            load_g(n)
-            if n == 0:
-                load_zeta()
-        warm_up(H, 5, 128)
-        factors()
-        turn("q", 0, 0, C)
-        turn("k", 0, 0, A)
-        turn("k", 0, 1, B)
-        turn("q", 0, 1, DD)
-        copy_k(0, 0)
-        copy_k(0, 1)
-        kd_on_gpsimd(0, 0)
-        for t in range(PACK):
-            widen_g(0, t)
+        load_rows(q, "q", 0, 0, 1)
+        load_rows(q, "q", 0, 1, 2)
+        load_g(0)
+        load_rows(k, "k", 0, 0, 2)
+        load_small("gk")
+        load_rows(k, "k", 0, 2, 4)
+        load_rows(q, "q", 0, 2, 4)
+        load_zeta()
+        load_rows(q, "q", 1, 0, 2)
+        load_rows(k, "k", 1, 0, 2)
+        load_rows(k, "k", 1, 2, 4)
+        load_rows(q, "q", 1, 2, 4)
+        load_g(1)
+        warm_up(H, 3, 128)
+        f_x()
+        f_t()
+        f_k()
+        turn("q", 0, 0, 1, G)
+        turn("q", 0, 1, 2, C)
+        warm_up(H, 1, 128)
+        turn("k", 0, 0, 2, A)
+        turn("k", 0, 2, 4, B)
+        turn("q", 0, 2, 4, DD)
+        widen_g(0, 0)
+        widen_g(0, 1)
+        copy_k(0, 0, 2)
+        kd_on_gpsimd(0, 0, 2)
+        widen_g(0, 2)
+        widen_g(0, 3)
         interleave_g(0)
-        scale_turned("x", "q", c_x, 0, 0)
-        scale_turned("p", "q", c_p, 0, 0)
-        scale_turned("kd", "k", c_k, 0, 1)
-        scale_turned("x", "q", c_x, 0, 1)
-        turn("k", 1, 0, A)
-        turn("k", 1, 1, B)
-        turn("q", 1, 0, C)
-        copy_k(1, 0)
-        copy_k(1, 1)
+        scale_turned("x", "q", c_x, 0, 0, 1)
+        f_p()
+        scale_turned("x", "q", c_x, 0, 1, 2)
+        scale_turned("p", "q", c_p, 0, 0, 1)
+        scale_turned("p", "q", c_p, 0, 1, 2)
+        scale_turned("kd", "k", c_k, 0, 2, 4)
+        copy_k(0, 2, 4)
+        scale_turned("x", "q", c_x, 0, 2, 4)
+        scale_turned("p", "q", c_p, 0, 2, 3)
+        turn("k", 1, 0, 2, A)
+        turn("q", 1, 0, 2, C)
+        turn("k", 1, 2, 4, B)
+        copy_k(1, 0, 2)
+        copy_k(1, 2, 4)
         quantize("kd", 0)
-        quantize("k", 0)
         quantize("x", 0)
-        zeta_factor()
         quantize("g", 0)
-        wide["kd", 1] = sbuf("kd_wide1", [P, 512 * PACK], BF16, tag="g_wide0")
-        kd_on_gpsimd(1, 0)
-        kd_on_gpsimd(1, 1)
+        zeta_factor()
+        quantize("k", 0)
+        wide["kd", 1] = sbuf("kd_wide1", [P, 512 * PACK], BF16, tag="k_wide0")
+        kd_on_gpsimd(1, 0, 2)
+        kd_on_gpsimd(1, 2, 4)
         widen_g(1, 0)
         widen_g(1, 1)
-        over_keys("s", "k", "x", 0, 0, EE)
-        over_keys("s", "k", "x", 0, 1, FF)
         over_keys("u", "kd", "g", 0, 0, A)
+        over_keys("s", "k", "x", 0, 0, EE)
         over_keys("u", "kd", "g", 0, 1, B)
+        over_keys("s", "k", "x", 0, 1, FF)
         over_keys("s", "k", "x", 0, 2, G)
         over_keys("s", "k", "x", 0, 3, H)
-        scale_turned("p", "q", c_p, 0, 1)
+        scale_turned("p", "q", c_p, 0, 3, 4)
         make_u(0, 0)
         make_u(0, 1)
         over_keys("u", "kd", "g", 0, 2, A)
         over_keys("u", "kd", "g", 0, 3, B)
         make_u(0, 2)
         make_u(0, 3)
-        turn("q", 1, 1, DD)
-        scale_turned("x", "q", c_x, 1, 0)
+        turn("q", 1, 2, 4, DD)
+        scale_turned("x", "q", c_x, 1, 0, 2)
         for b in range(PACK):
             make_sz(0, b)
-        scale_turned("x", "q", c_x, 1, 1)
+        scale_turned("x", "q", c_x, 1, 2, 4)
+        scale_turned("p", "q", c_p, 1, 0, 1)
         widen_g(1, 2)
         widen_g(1, 3)
         interleave_g(1)
+        p_planes(1, 1, 2)
+        p_planes(1, 2, 3)
         rewarm(A, 3)
         quantize("kd", 1)
         quantize("p", 0)
@@ -369,52 +392,54 @@ def tile_diagonalpreconditionedstepread_kernel(tc, q, k, zeta, lam, g_bytes, g_s
         quantize("g", 1)
         quantize("k", 1)
         quantize("x", 1)
+        p_interleave(1, 1, 2)
+        p_interleave(1, 2, 3)
         for b, index in enumerate((EE, FF, G, H)):
             out_open(0, b, index)
-        for b in range(PACK):
-            out_close(0, b)
+        out_close(0, 0)
+        out_close(0, 1)
         over_keys("u", "kd", "g", 1, 0, A)
         over_keys("u", "kd", "g", 1, 1, B)
         store(0, 0)
         store(0, 1)
+        over_keys("s", "k", "x", 1, 0, C)
         over_keys("u", "kd", "g", 1, 2, EE)
-        over_keys("u", "kd", "g", 1, 3, FF)
+        over_keys("s", "k", "x", 1, 1, FF)
         make_u(1, 0)
+        over_keys("u", "kd", "g", 1, 3, A)
         make_u(1, 1)
-        over_keys("s", "k", "x", 1, 0, A)
-        over_keys("s", "k", "x", 1, 1, B)
+        out_close(0, 2)
+        out_close(0, 3)
         make_u(1, 2)
         make_u(1, 3)
-        over_keys("s", "k", "x", 1, 2, EE)
-        over_keys("s", "k", "x", 1, 3, FF)
+        over_keys("s", "k", "x", 1, 2, B)
+        over_keys("s", "k", "x", 1, 3, EE)
         store(0, 2)
         store(0, 3)
-        scale_turned("p", "q", c_p, 1, 0)
-        scale_turned("p", "q", c_p, 1, 1)
-        make_sz(1, 0)
-        quantize("p", 1)
-        quantize("u", 1)
-        quantize("sz", 1, 0, 128)
-        make_sz(1, 1)
-        sz_planes(1, 2)
         sz_planes(1, 3)
+        make_sz(1, 0)
+        make_sz(1, 1)
+        quantize("p", 1, 0, 2)
+        quantize("p", 1, 2, 3)
+        quantize("u", 1)
+        quantize("sz", 1, 0, 2)
         out_open(1, 0, C)
-        out_open(1, 1, DD)
+        out_open(1, 1, FF)
         out_close(1, 0)
-        out_open(1, 2, G)
-        out_open_half(1, 3, 0, H)
-        out_open_half(1, 3, 1, A)
-        sz_interleave(1, 2)
-        quantize("sz", 1, 128, 256)
-        sz_interleave(1, 3)
-        quantize("sz", 1, 256, 384)
-        quantize("sz", 1, 384, 512)
         out_close(1, 1)
-        out_close(1, 2)
+        make_sz(1, 2)
+        scale_turned("p", "q", c_p, 1, 3, 4)
+        quantize("sz", 1, 2, 3)
+        out_product(1, 2, A)
+        sz_interleave(1, 3)
+        quantize("p", 1, 3, 4)
+        quantize("sz", 1, 3, 4)
+        out_open_half(1, 3, 0, G)
+        out_open_half(1, 3, 1, H)
         out_close_half(1, 3, 0)
         out_close_half(1, 3, 1)
         store(1, 0)
         store(1, 1)
-        store(1, 2, "V")
-        store_half(1, 3, 0)
-        store_half(1, 3, 1, "V")
+        store(1, 2)
+        store_half(1, 3, 0, "V")
+        store_half(1, 3, 1)

@@ -54,6 +54,8 @@ def tile_diagonalpreconditionedstepread_kernel(tc, q, k, zeta, lam, g_bytes, g_s
 
         nc.scalar.dma_start(out=gs_sb[:], in_=g_scale.rearrange("a (p t) b -> p (a t b)", t=PACK))
 
+        nc.scalar.dma_start(out=gk_sb[:], in_=gk.rearrange("(p t) -> p t", t=PACK))
+
         rows = {}
         g_raw = {}
 
@@ -101,7 +103,7 @@ def tile_diagonalpreconditionedstepread_kernel(tc, q, k, zeta, lam, g_bytes, g_s
             nc.vector.tensor_tensor(out=c_p[:], in0=c_t[:], in1=gq_sb[:], op=MULT)
 
         def f_k():
-            nc.gpsimd.tensor_tensor(out=c_k[:], in0=c_x[:], in1=gk_sb[:], op=MULT)
+            nc.vector.tensor_tensor(out=c_k[:], in0=c_x[:], in1=gk_sb[:], op=MULT)
 
         def zeta_factor():
             nc.vector.tensor_scalar(out=c_z[:], in0=zeta_sb[:], scalar1=INV_ROOT_D, scalar2=None, op0=MULT)
@@ -295,13 +297,13 @@ def tile_diagonalpreconditionedstepread_kernel(tc, q, k, zeta, lam, g_bytes, g_s
             nc.sync.dma_start(out=dst[:, HALF * hh : HALF * (hh + 1)], in_=res[:])
 
         def warm_up(index, count, width):
-            acc = bank(index, "warm_sums%d" % count)
+            acc = bank(index, "warm_sums%d%d" % (index, count))
             for i in range(count):
                 nc.tensor.matmul(acc[:, :width], lhsT=zeros[:], rhs=zeros[:], start=True, stop=True)
 
-        def rewarm(index, count):
-            src = slots("kd", 1, 2, 4)
-            acc = bank(index, "rewarm_sums")
+        def rewarm(name, n, index, count):
+            src = slots(name, n, 2, 4)
+            acc = bank(index, "rewarm_sums%d" % n)
             for i in range(count):
                 nc.tensor.matmul(acc[:], lhsT=src[:, :P], rhs=src[:, :512], start=True, stop=True)
 
@@ -310,7 +312,6 @@ def tile_diagonalpreconditionedstepread_kernel(tc, q, k, zeta, lam, g_bytes, g_s
         load_rows(q, "q", 0, 1, 2)
         load_g(0)
         load_rows(k, "k", 0, 0, 2)
-        load_small("gk")
         load_rows(k, "k", 0, 2, 4)
         load_rows(q, "q", 0, 2, 4)
         load_zeta()
@@ -319,25 +320,26 @@ def tile_diagonalpreconditionedstepread_kernel(tc, q, k, zeta, lam, g_bytes, g_s
         load_rows(k, "k", 1, 2, 4)
         load_rows(q, "q", 1, 2, 4)
         load_g(1)
-        warm_up(H, 3, 128)
+        warm_up(H, 4, 128)
         f_x()
         f_t()
-        f_k()
         turn("q", 0, 0, 1, G)
         turn("q", 0, 1, 2, C)
-        warm_up(H, 1, 128)
+        warm_up(H, 2, 128)
         turn("k", 0, 0, 2, A)
         turn("k", 0, 2, 4, B)
         turn("q", 0, 2, 4, DD)
+        warm_up(EE, 2, 128)
         widen_g(0, 0)
         widen_g(0, 1)
         copy_k(0, 0, 2)
+        scale_turned("x", "q", c_x, 0, 0, 1)
+        f_p()
+        f_k()
         kd_on_gpsimd(0, 0, 2)
         widen_g(0, 2)
         widen_g(0, 3)
         interleave_g(0)
-        scale_turned("x", "q", c_x, 0, 0, 1)
-        f_p()
         scale_turned("x", "q", c_x, 0, 1, 2)
         scale_turned("p", "q", c_p, 0, 0, 1)
         scale_turned("p", "q", c_p, 0, 1, 2)
@@ -345,9 +347,11 @@ def tile_diagonalpreconditionedstepread_kernel(tc, q, k, zeta, lam, g_bytes, g_s
         copy_k(0, 2, 4)
         scale_turned("x", "q", c_x, 0, 2, 4)
         scale_turned("p", "q", c_p, 0, 2, 3)
-        turn("k", 1, 0, 2, A)
         turn("q", 1, 0, 2, C)
-        turn("k", 1, 2, 4, B)
+        turn("k", 1, 0, 2, A)
+        turn("k", 1, 2, 4, G)
+        turn("q", 1, 2, 4, H)
+        rewarm("k", 0, EE, 2)
         copy_k(1, 0, 2)
         copy_k(1, 2, 4)
         quantize("kd", 0)
@@ -364,16 +368,15 @@ def tile_diagonalpreconditionedstepread_kernel(tc, q, k, zeta, lam, g_bytes, g_s
         over_keys("s", "k", "x", 0, 0, EE)
         over_keys("u", "kd", "g", 0, 1, B)
         over_keys("s", "k", "x", 0, 1, FF)
-        over_keys("s", "k", "x", 0, 2, G)
-        over_keys("s", "k", "x", 0, 3, H)
         scale_turned("p", "q", c_p, 0, 3, 4)
         make_u(0, 0)
         make_u(0, 1)
         over_keys("u", "kd", "g", 0, 2, A)
+        over_keys("s", "k", "x", 0, 2, G)
         over_keys("u", "kd", "g", 0, 3, B)
+        over_keys("s", "k", "x", 0, 3, DD)
         make_u(0, 2)
         make_u(0, 3)
-        turn("q", 1, 2, 4, DD)
         scale_turned("x", "q", c_x, 1, 0, 2)
         for b in range(PACK):
             make_sz(0, b)
@@ -384,58 +387,43 @@ def tile_diagonalpreconditionedstepread_kernel(tc, q, k, zeta, lam, g_bytes, g_s
         interleave_g(1)
         p_planes(1, 1, 2)
         p_planes(1, 2, 3)
-        rewarm(A, 3)
+        rewarm("kd", 1, A, 3)
+        quantize("k", 1)
+        quantize("x", 1)
         quantize("kd", 1)
+        quantize("g", 1)
         quantize("p", 0)
         quantize("sz", 0)
         quantize("u", 0)
-        quantize("g", 1)
-        quantize("k", 1)
-        quantize("x", 1)
         p_interleave(1, 1, 2)
         p_interleave(1, 2, 3)
-        for b, index in enumerate((EE, FF, G, H)):
-            out_open(0, b, index)
-        out_close(0, 0)
-        out_close(0, 1)
-        over_keys("u", "kd", "g", 1, 0, A)
-        over_keys("u", "kd", "g", 1, 1, B)
-        store(0, 0)
-        store(0, 1)
-        over_keys("s", "k", "x", 1, 0, C)
-        over_keys("u", "kd", "g", 1, 2, EE)
-        over_keys("s", "k", "x", 1, 1, FF)
-        make_u(1, 0)
-        over_keys("u", "kd", "g", 1, 3, A)
-        make_u(1, 1)
-        out_close(0, 2)
-        out_close(0, 3)
-        make_u(1, 2)
-        make_u(1, 3)
-        over_keys("s", "k", "x", 1, 2, B)
-        over_keys("s", "k", "x", 1, 3, EE)
-        store(0, 2)
-        store(0, 3)
-        sz_planes(1, 3)
+        for b, index in enumerate((EE, FF, G, DD)):
+            over_keys("s", "k", "x", 1, b, index)
+        for b, index in enumerate((A, B, C, A)):
+            over_keys("u", "kd", "g", 1, b, index)
+            make_u(1, b)
         make_sz(1, 0)
         make_sz(1, 1)
+        for b, index in enumerate((B, C, A, EE)):
+            out_product(0, b, index)
+            store(0, b)
         quantize("p", 1, 0, 2)
-        quantize("p", 1, 2, 3)
         quantize("u", 1)
         quantize("sz", 1, 0, 2)
-        out_open(1, 0, C)
-        out_open(1, 1, FF)
+        out_open(1, 0, FF)
+        out_open(1, 1, B)
         out_close(1, 0)
         out_close(1, 1)
         make_sz(1, 2)
-        scale_turned("p", "q", c_p, 1, 3, 4)
+        quantize("p", 1, 2, 3)
         quantize("sz", 1, 2, 3)
-        out_product(1, 2, A)
-        sz_interleave(1, 3)
+        out_product(1, 2, C)
+        scale_turned("p", "q", c_p, 1, 3, 4)
+        make_sz(1, 3)
         quantize("p", 1, 3, 4)
         quantize("sz", 1, 3, 4)
-        out_open_half(1, 3, 0, G)
-        out_open_half(1, 3, 1, H)
+        out_open_half(1, 3, 0, A)
+        out_open_half(1, 3, 1, EE)
         out_close_half(1, 3, 0)
         out_close_half(1, 3, 1)
         store(1, 0)

import math
from contextlib import ExitStack

import concourse.mybir as mybir
from concourse.masks import make_identity

N, T, D, E = 2, 512, 512, 512
FLOPS = N * 2 * (T * T * D + 2 * T * D * E + T * T * E)

F32 = mybir.dt.float32
BF16 = mybir.dt.bfloat16
U32 = mybir.dt.uint32
U8 = mybir.dt.uint8
FP8 = mybir.dt.float8_e4m3fn
FP8X4 = mybir.dt.float8_e4m3fn_x4
MULT = mybir.AluOpType.mult
ADD = mybir.AluOpType.add
COPY = mybir.ActivationFunctionType.Copy

P = 128
PACK = 4
HALF = 256
CHUNK = 128
INV_ROOT_D = 1.0 / math.sqrt(D)

LATE = (("kd", 1), ("q", 0), ("q", 1))

assert T == D == E == P * PACK


def tile_diagonalpreconditionedstepread_kernel(tc, q, k, zeta, lam, g_bytes, g_scale, gk, gq, out):
    nc = tc.nc
    with ExitStack() as ctx:
        keep = ctx.enter_context(tc.tile_pool(name="keep", bufs=1))
        psum = ctx.enter_context(tc.psum_pool(name="psum", bufs=1))
        ctx.enter_context(tc.manual_schedule())

        def sbuf(name, shape, dtype, tag=None):
            return keep.tile(shape, dtype, name=name, tag=tag or name, align_bytes=64)

        def bank(index, name):
            return psum.tile([P, 512], F32, name=name, tag="bank%d" % index)

        def mx_operand(name):
            return sbuf(name + "_codes", [P, 512], U32), sbuf(name + "_scales", [P, 512], U8)

        lam_sb = sbuf("lam_sb", [P, PACK], BF16)
        gk_sb = sbuf("gk_sb", [P, PACK], BF16)
        gq_sb = sbuf("gq_sb", [P, PACK], BF16)
        gs_sb = sbuf("gs_sb", [P, PACK], F32)
        zeta_sb = sbuf("zeta_sb", [P, N, PACK], BF16)
        nc.scalar.dma_start(out=lam_sb[:], in_=lam.rearrange("(p t) -> p t", t=PACK))
        nc.scalar.dma_start(out=gq_sb[:], in_=gq.rearrange("(p t) -> p t", t=PACK))

        nc.scalar.dma_start(out=gs_sb[:], in_=g_scale.rearrange("a (p t) b -> p (a t b)", t=PACK))

        nc.scalar.dma_start(out=gk_sb[:], in_=gk.rearrange("(p t) -> p t", t=PACK))

        rows = {}
        g_raw = {}

        def load_rows(src, name, n, j0, j1):
            t = sbuf("%s_rows%d%d" % (name, n, j0), [P, (j1 - j0) * D], BF16)
            nc.sync.dma_start(out=t[:], in_=src[n].rearrange("(m j) d -> m (j d)", j=PACK)[:, D * j0 : D * j1])
            rows[name, n, j0] = t

        def load_small(which):
            if which == "gk":
                nc.sync.dma_start(out=gk_sb[:], in_=gk.rearrange("(p t) -> p t", t=PACK))
            else:
                nc.sync.dma_start(out=gs_sb[:], in_=g_scale.rearrange("a (p t) b -> p (a t b)", t=PACK))

        def load_g(n):
            t = sbuf("g_raw%d" % n, [P, PACK * E], U8)
            nc.sync.dma_start(out=t[:], in_=g_bytes[n].rearrange("(p t) e -> p (t e)", t=PACK))
            g_raw[n] = t

        def load_zeta():
            nc.sync.dma_start(out=zeta_sb[:], in_=zeta.rearrange("n (p j) -> p n j", j=PACK))

        zeros = sbuf("warm_zeros", [P, P], F32)
        nc.gpsimd.memset(zeros[:], 0.0)
        ident = sbuf("ident", [P, P], F32)
        make_identity(nc, ident[:])
        warm = sbuf("warm", [P, 1], F32)
        nc.scalar.activation(out=warm[:], in_=ident[:, 0:1], func=COPY, scale=1.0)

        dg = sbuf("dg", [P, PACK], F32)
        c_x = sbuf("c_x", [P, PACK], F32)
        c_k = sbuf("c_k", [P, PACK], F32)
        c_t = sbuf("c_t", [P, PACK], F32)
        c_p = sbuf("c_p", [P, PACK], F32)
        c_z = sbuf("c_z", [P, N, PACK], F32)

        def f_x():
            nc.vector.tensor_scalar(out=dg[:], in0=lam_sb[:], scalar1=1.0, scalar2=None, op0=ADD)
            nc.vector.reciprocal(out=c_x[:], in_=dg[:])

        def f_t():
            nc.vector.scalar_tensor_tensor(out=c_t[:], in0=c_x[:], scalar=1.0, in1=c_x[:], op0=ADD, op1=MULT)

        def f_p():
            nc.vector.tensor_tensor(out=c_p[:], in0=c_t[:], in1=gq_sb[:], op=MULT)

        def f_k():
            nc.vector.tensor_tensor(out=c_k[:], in0=c_x[:], in1=gk_sb[:], op=MULT)

        def zeta_factor():
            nc.vector.tensor_scalar(out=c_z[:], in0=zeta_sb[:], scalar1=INV_ROOT_D, scalar2=None, op0=MULT)

        wide = {}
        mx = {}
        for n in range(N):
            for name in ("k", "x", "p", "kd", "g", "sz", "u"):
                mx[name, n] = mx_operand("%s%d" % (name, n))
            for name in ("k", "q", "x", "p", "sz", "u", "kd", "g"):
                if (name, n) not in LATE:
                    wide[name, n] = sbuf("%s_wide%d" % (name, n), [P, 512 * PACK], BF16)
        planes = {n: sbuf("g_planes%d" % n, [P, PACK, E], BF16) for n in range(N)}
        turned = {}
        sums = {}

        def turn(name, n, j0, j1, index):
            b = bank(index, "%s_turned%d%d" % (name, n, j0))
            words = rows[name, n, j0][:].bitcast(F32)
            view = b[:].rearrange("p (u c) -> p c u", u=2)
            for j in range(j1 - j0):
                for u in range(2):
                    nc.tensor.transpose(
                        b[:, HALF * u + P * j : HALF * u + P * (j + 1)],
                        words[:, HALF * j + u : HALF * (j + 1) : 2],
                        ident[:],
                    )
                turned[name, n, j0 + j] = (b, j)

        def slots(name, n, j0, j1):
            return wide[name, n][:, P * PACK * j0 : P * PACK * j1]

        def turned_values(name, n, j0, j1):
            b, first = turned[name, n, j0]
            view = b[:].bitcast(BF16).rearrange("p (u c e) -> p c u e", u=2, e=2)
            return view[:, P * first : P * (first + j1 - j0)]

        def copy_k(n, j0, j1):
            b, first = turned["k", n, j0]
            nc.scalar.copy(
                out=slots("k", n, j0, j1).bitcast(F32).rearrange("p (c u) -> p c u", u=2),
                in_=b[:].rearrange("p (u c) -> p c u", u=2)[:, P * first : P * (first + j1 - j0)],
            )

        def scale_turned(dst, src, factor, n, j0, j1):
            nc.vector.tensor_tensor(
                out=slots(dst, n, j0, j1).rearrange("p (c u e) -> p c u e", u=2, e=2),
                in0=turned_values(src, n, j0, j1),
                in1=factor[:].rearrange("p (u e) -> p u e", u=2).unsqueeze(1).to_broadcast([P, P * (j1 - j0), 2, 2]),
                op=MULT,
            )

        def kd_on_gpsimd(n, j0, j1):
            nc.gpsimd.tensor_tensor(
                out=slots("kd", n, j0, j1).rearrange("p (c t) -> p c t", t=PACK),
                in0=slots("k", n, j0, j1).rearrange("p (c t) -> p c t", t=PACK),
                in1=c_k[:].unsqueeze(1).to_broadcast([P, P * (j1 - j0), PACK]),
                op=MULT,
            )

        t_planes = {}

        def p_planes(n, j0, j1):
            pl = sbuf("p_planes%d%d" % (n, j0), [P, PACK, P * (j1 - j0)], BF16)
            view = turned_values("q", n, j0, j1)
            for t in range(PACK):
                nc.scalar.activation(
                    out=pl[:, t, :], in_=view[:, :, t // 2, t % 2], func=COPY, scale=c_p[:, t : t + 1]
                )
            t_planes[n, j0] = pl

        def p_interleave(n, j0, j1):
            nc.vector.tensor_copy(
                out=slots("p", n, j0, j1).rearrange("p (c i t) -> p c t i", i=4, t=PACK),
                in_=t_planes[n, j0][:].rearrange("p t (c i) -> p c t i", i=4),
            )

        def widen_g(n, t, eng="S"):
            src = g_raw[n][:, E * t : E * (t + 1)].bitcast(FP8)
            if eng == "S":
                nc.scalar.activation(out=planes[n][:, t, :], in_=src, func=COPY, scale=gs_sb[:, t : t + 1])
            else:
                nc.vector.tensor_scalar(
                    out=planes[n][:, t, :], in0=src, scalar1=gs_sb[:, t : t + 1], scalar2=None, op0=MULT
                )

        def interleave_g(n, c0=0, c1=512, eng="S"):
            dst = wide["g", n][:, PACK * c0 : PACK * c1].rearrange("p (c i t) -> p c t i", i=4, t=PACK)
            src = planes[n][:, :, c0:c1].rearrange("p t (c i) -> p c t i", i=4)
            if eng == "S":
                nc.scalar.copy(out=dst, in_=src)
            elif eng == "V":
                nc.vector.tensor_copy(out=dst, in_=src)
            else:
                nc.gpsimd.tensor_scalar(out=dst, in0=src, scalar1=1.0, scalar2=0.0, op0=MULT, op1=ADD)

        def quantize(name, n, j0=0, j1=PACK):
            codes, scales = mx[name, n]
            nc.vector.quantize_mx(
                out=codes[:, P * j0 : P * j1].bitcast(FP8X4),
                scales=scales[:, P * j0 : P * j1],
                in_=slots(name, n, j0, j1),
            )

        def mx_pass(dst, lhs, rhs, n, m_cols, n_cols, start, stop):
            nc.tensor.matmul_mx(
                out=dst,
                lhsT=mx[lhs, n][0][:, m_cols].bitcast(FP8X4),
                lhsT_scale=mx[lhs, n][1][:, m_cols],
                rhs=mx[rhs, n][0][:, n_cols].bitcast(FP8X4),
                rhs_scale=mx[rhs, n][1][:, n_cols],
                start=start,
                stop=stop,
            )

        def cols(b):
            return slice(CHUNK * b, CHUNK * (b + 1))

        def over_keys(name, lhs, rhs, n, b, index):
            acc = bank(index, "%s_sums%d%d" % (name, n, b))
            for j in range(PACK):
                mx_pass(acc[:, cols(j)], lhs, rhs, n, cols(j), cols(b), True, True)
            sums[name, n, b] = acc

        def chunk(name, n, b):
            return wide[name, n][:, CHUNK * PACK * b : CHUNK * PACK * (b + 1)].rearrange("p (c j) -> p c j", j=PACK)

        def make_sz(n, b):
            nc.vector.tensor_tensor(
                out=chunk("sz", n, b),
                in0=sums["s", n, b][:].rearrange("p (j c) -> p c j", j=PACK),
                in1=c_z[:, n, :].unsqueeze(1).to_broadcast([P, CHUNK, PACK]),
                op=MULT,
            )

        z_planes = {}

        def sz_planes(n, b):
            pl = sbuf("z_planes%d%d" % (n, b), [P, PACK, CHUNK], BF16)
            for j in range(PACK):
                nc.scalar.activation(
                    out=pl[:, j, :], in_=sums["s", n, b][:, cols(j)], func=COPY, scale=c_z[:, n, j : j + 1]
                )
            z_planes[n, b] = pl

        def sz_interleave(n, b):
            nc.vector.tensor_copy(
                out=chunk("sz", n, b).rearrange("p (c i) t -> p c t i", i=4),
                in_=z_planes[n, b][:].rearrange("p t (c i) -> p c t i", i=4),
            )

        def scaled_copy(dst, src, factor, eng):
            if eng == "S":
                nc.scalar.activation(out=dst, in_=src, func=COPY, scale=factor)
            else:
                nc.vector.tensor_scalar(out=dst, in0=src, scalar1=factor, scalar2=None, op0=MULT)

        def make_u(n, b, eng="S"):
            scaled_copy(chunk("u", n, b), sums["u", n, b][:].rearrange("p (j c) -> p c j", j=PACK), -INV_ROOT_D, eng)

        def out_open(n, b, index):
            acc = bank(index, "out_sums%d%d" % (n, b))
            mx_pass(acc[:], "p", "g", n, cols(b), slice(0, E), True, False)
            sums["out", n, b] = acc

        def out_close(n, b):
            mx_pass(sums["out", n, b][:], "sz", "u", n, cols(b), slice(0, E), False, True)

        def out_product(n, b, index):
            out_open(n, b, index)
            out_close(n, b)

        def store(n, b, eng="S"):
            res = sbuf("res%d%d" % (n, b), [P, E], F32)
            scaled_copy(res[:], sums["out", n, b][:], INV_ROOT_D, eng)
            nc.sync.dma_start(out=out[n].rearrange("(m j) e -> j m e", j=PACK)[b], in_=res[:])

        def out_open_half(n, b, hh, index):
            acc = bank(index, "out_sums%d%d%d" % (n, b, hh))
            mx_pass(acc[:, :HALF], "p", "g", n, cols(b), slice(HALF * hh, HALF * (hh + 1)), True, False)
            sums["out", n, b, hh] = acc

        def out_close_half(n, b, hh):
            acc = sums["out", n, b, hh]
            mx_pass(acc[:, :HALF], "sz", "u", n, cols(b), slice(HALF * hh, HALF * (hh + 1)), False, True)

        def store_half(n, b, hh, eng="S"):
            res = sbuf("res%d%d%d" % (n, b, hh), [P, HALF], F32)
            scaled_copy(res[:], sums["out", n, b, hh][:, :HALF], INV_ROOT_D, eng)
            dst = out[n].rearrange("(m j) e -> j m e", j=PACK)[b]
            nc.sync.dma_start(out=dst[:, HALF * hh : HALF * (hh + 1)], in_=res[:])

        def warm_up(index, count, width):
            acc = bank(index, "warm_sums%d%d" % (index, count))
            for i in range(count):
                nc.tensor.matmul(acc[:, :width], lhsT=zeros[:], rhs=zeros[:], start=True, stop=True)

        def rewarm(name, n, index, count):
            src = slots(name, n, 2, 4)
            acc = bank(index, "rewarm_sums%d" % n)
            for i in range(count):
                nc.tensor.matmul(acc[:], lhsT=src[:, :P], rhs=src[:, :512], start=True, stop=True)

        A, B, C, DD, EE, FF, G, H = range(8)
        load_rows(q, "q", 0, 0, 1)
        load_rows(q, "q", 0, 1, 2)
        load_g(0)
        load_rows(k, "k", 0, 0, 2)
        load_rows(k, "k", 0, 2, 4)
        load_rows(q, "q", 0, 2, 4)
        load_zeta()
        load_rows(q, "q", 1, 0, 2)
        load_rows(k, "k", 1, 0, 2)
        load_rows(k, "k", 1, 2, 4)
        load_rows(q, "q", 1, 2, 4)
        load_g(1)
        warm_up(H, 4, 128)
        f_x()
        f_t()
        turn("q", 0, 0, 1, G)
        turn("q", 0, 1, 2, C)
        warm_up(H, 2, 128)
        turn("k", 0, 0, 2, A)
        turn("k", 0, 2, 4, B)
        turn("q", 0, 2, 4, DD)
        warm_up(EE, 2, 128)
        widen_g(0, 0)
        widen_g(0, 1)
        copy_k(0, 0, 2)
        scale_turned("x", "q", c_x, 0, 0, 1)
        f_p()
        f_k()
        kd_on_gpsimd(0, 0, 2)
        widen_g(0, 2)
        widen_g(0, 3)
        interleave_g(0)
        scale_turned("x", "q", c_x, 0, 1, 2)
        scale_turned("p", "q", c_p, 0, 0, 1)
        scale_turned("p", "q", c_p, 0, 1, 2)
        scale_turned("kd", "k", c_k, 0, 2, 4)
        copy_k(0, 2, 4)
        scale_turned("x", "q", c_x, 0, 2, 4)
        scale_turned("p", "q", c_p, 0, 2, 3)
        turn("q", 1, 0, 2, C)
        turn("k", 1, 0, 2, A)
        turn("k", 1, 2, 4, G)
        turn("q", 1, 2, 4, H)
        rewarm("k", 0, EE, 2)
        copy_k(1, 0, 2)
        copy_k(1, 2, 4)
        quantize("kd", 0)
        quantize("x", 0)
        quantize("g", 0)
        zeta_factor()
        quantize("k", 0)
        wide["kd", 1] = sbuf("kd_wide1", [P, 512 * PACK], BF16, tag="k_wide0")
        kd_on_gpsimd(1, 0, 2)
        kd_on_gpsimd(1, 2, 4)
        widen_g(1, 0)
        widen_g(1, 1)
        over_keys("u", "kd", "g", 0, 0, A)
        over_keys("s", "k", "x", 0, 0, EE)
        over_keys("u", "kd", "g", 0, 1, B)
        over_keys("s", "k", "x", 0, 1, FF)
        scale_turned("p", "q", c_p, 0, 3, 4)
        make_u(0, 0)
        make_u(0, 1)
        over_keys("u", "kd", "g", 0, 2, A)
        over_keys("s", "k", "x", 0, 2, G)
        over_keys("u", "kd", "g", 0, 3, B)
        over_keys("s", "k", "x", 0, 3, DD)
        make_u(0, 2)
        make_u(0, 3)
        scale_turned("x", "q", c_x, 1, 0, 2)
        for b in range(PACK):
            make_sz(0, b)
        scale_turned("x", "q", c_x, 1, 2, 4)
        scale_turned("p", "q", c_p, 1, 0, 1)
        widen_g(1, 2)
        widen_g(1, 3)
        interleave_g(1)
        p_planes(1, 1, 2)
        p_planes(1, 2, 3)
        rewarm("kd", 1, A, 3)
        quantize("k", 1)
        quantize("x", 1)
        quantize("kd", 1)
        quantize("g", 1)
        quantize("p", 0)
        quantize("sz", 0)
        quantize("u", 0)
        p_interleave(1, 1, 2)
        p_interleave(1, 2, 3)
        for b, index in enumerate((EE, FF, G, DD)):
            over_keys("s", "k", "x", 1, b, index)
        for b, index in enumerate((A, B, C, A)):
            over_keys("u", "kd", "g", 1, b, index)
            make_u(1, b)
        make_sz(1, 0)
        make_sz(1, 1)
        for b, index in enumerate((B, C, A, EE)):
            out_product(0, b, index)
            store(0, b)
        quantize("p", 1, 0, 2)
        quantize("u", 1)
        quantize("sz", 1, 0, 2)
        out_open(1, 0, FF)
        out_open(1, 1, B)
        out_close(1, 0)
        out_close(1, 1)
        make_sz(1, 2)
        quantize("p", 1, 2, 3)
        quantize("sz", 1, 2, 3)
        out_product(1, 2, C)
        scale_turned("p", "q", c_p, 1, 3, 4)
        make_sz(1, 3)
        quantize("p", 1, 3, 4)
        quantize("sz", 1, 3, 4)
        out_open_half(1, 3, 0, A)
        out_open_half(1, 3, 1, EE)
        out_close_half(1, 3, 0)
        out_close_half(1, 3, 1)
        store(1, 0)
        store(1, 1)
        store(1, 2)
        store_half(1, 3, 0, "V")
        store_half(1, 3, 1)
